import numpy as np
import ml_dtypes


def mxq(x, axis, fmt="e4m3"):
    dtype, down = {"e4m3": (ml_dtypes.float8_e4m3fn, 7), "e5m2": (ml_dtypes.float8_e5m2, 14)}[fmt]
    v = np.moveaxis(np.asarray(x, np.float32).astype(ml_dtypes.bfloat16).astype(np.float64), axis, -1)
    blocks = v.reshape(v.shape[:-1] + (-1, 32))
    amax = np.abs(blocks).max(-1, keepdims=True)
    byte = np.maximum(np.where(amax > 0, np.frexp(amax)[1] - 1 + 127, 0) - down, 1)
    scale = np.exp2(byte - 127.0)
    codes = (blocks / scale).astype(np.float32).astype(dtype).astype(np.float64)
    return np.moveaxis((codes * scale).reshape(v.shape), -1, axis)


WIDE = False


def mx_kscale(k, group=512):
    if not WIDE:
        return np.ones(k)
    levels = np.array([10, -10, 5, -5, 0])
    if group != 512:
        return np.exp2(np.random.permutation(np.resize(levels, k // group))).repeat(group)
    if k % 512:
        return np.exp2(np.random.permutation(np.resize(levels, k // 32))).repeat(32)
    a = np.empty((k // 512, 16))
    for p in range(k // 512):
        a[p, :8] = np.random.permutation(np.resize(levels, 8))
        for g in range(8):
            far = levels[np.abs(levels - a[p, g]) >= 10]
            a[p, g + 8] = far[np.random.randint(len(far))]
    return np.exp2(a.ravel()).repeat(32)


def f64(x):
    return np.asarray(x).astype(np.float64)


K, R, M, N = 512, 256, 512, 1024


def setup_inputs():
    n = np.random.standard_normal
    s = mx_kscale(K)[:, None]
    z = mx_kscale(R, 0)
    return {
        "x": (n((K, N)) * s).astype(np.float32),
        "w": (n((K, M)) / np.sqrt(K) / s).astype(np.float32),
        "a": (n((K, R)) / np.sqrt(K) / s * z).astype(np.float32),
        "bb": (n((R, M)) / np.sqrt(R) / z[:, None]).astype(np.float32),
    }


def reference(x, w, a, bb):
    xq = mxq(f64(x), 0, "e4m3")
    z = mxq(f64(a), 0, "e4m3").T @ xq
    y = (mxq(f64(w), 0, "e4m3").T @ xq) + (mxq(f64(bb), 0, "e4m3").T @ mxq(z, 0, "e4m3"))
    y = np.maximum(y, 0.0)
    return y

@@ -1,0 +1,244 @@
+from contextlib import ExitStack
+
+import concourse.mybir as mybir
+
+K, R, M, N = 512, 256, 512, 1024
+FLOPS = 2 * N * (K * M + K * R + R * M)
+
+F32 = mybir.dt.float32
+BF16 = mybir.dt.bfloat16
+I32 = mybir.dt.int32
+U32 = mybir.dt.uint32
+U8 = mybir.dt.uint8
+FP8X4 = mybir.dt.float8_e4m3fn_x4
+ALU = mybir.AluOpType
+ACT = mybir.ActivationFunctionType
+
+P = 128
+PACK = 4
+ROWS = 64
+NT = 128
+CHUNK = 2 * NT
+CHUNKS = N // CHUNK
+MT = M // P
+HALF_M = M // 2
+
+W_CODES = 0
+W_SCALES = W_CODES + M * PACK
+BB_CODES = W_SCALES + M
+BB_SCALES = BB_CODES + HALF_M * PACK
+WB_BYTES = BB_SCALES + HALF_M
+X_SCALES = NT * PACK
+X_BYTES = X_SCALES + NT
+
+BB_SPLIT = 176
+A_SPLIT = 44
+W_SPLIT = 336
+
+
+def tile_rows_lora_relu_kernel(tc, x, w, a, bb, out):
+    nc = tc.nc
+
+    def interleave(dst, src, split):
+        cols = src.shape[2]
+        for lo, hi, copy in ((0, split, nc.vector.tensor_copy), (split, cols, nc.scalar.copy)):
+            if hi > lo:
+                copy(
+                    out=dst[:, lo:hi, :].rearrange("p (c i) j -> p c j i", i=4),
+                    in_=src[:, :, lo:hi].rearrange("p j (c i) -> p c j i", i=4),
+                )
+
+    def quantize(codes, scales, grouped):
+        nc.vector.quantize_mx(out=codes.bitcast(FP8X4), scales=scales, in_=grouped)
+
+    with ExitStack() as ctx:
+        sb = ctx.enter_context(tc.tile_pool(name="sb", bufs=1))
+        ps = ctx.enter_context(tc.psum_pool(name="ps", bufs=1))
+        ctx.enter_context(tc.manual_schedule())
+
+        bb_raw = sb.tile([P, PACK, HALF_M], F32, name="bb_raw")
+        bb_bf = sb.tile([P, HALF_M, PACK], BF16, name="bb_bf", align_bytes=64)
+        wb_mx = sb.tile([P, 2, WB_BYTES], U8, name="wb_mx", align_bytes=64)
+        a_raw = sb.tile([P, PACK, R], F32, name="a_raw")
+        a_bf = sb.tile([P, PACK, ROWS, PACK], BF16, name="a_bf", align_bytes=64)
+        a_codes = sb.tile([P, (2 * PACK + 1) * ROWS], U32, name="a_codes", align_bytes=64)
+        a_scales = sb.tile([P, (2 * PACK + 1) * ROWS], U8, name="a_scales", align_bytes=64)
+        w_raw = sb.tile([P, PACK, M], F32, name="w_raw")
+        w_bf = sb.tile([P, M, PACK], BF16, name="w_bf", align_bytes=64)
+        x_raw = [sb.tile([P, PACK, CHUNK], F32, name="x_raw%d" % q) for q in range(CHUNKS)]
+        x_bf = [sb.tile([P, CHUNK, PACK], BF16, name="x_bf%d" % q, align_bytes=64) for q in range(CHUNKS)]
+        x_mx = [sb.tile([P, 3, X_BYTES], U8, name="x_mx%d" % q, align_bytes=64) for q in range(CHUNKS)]
+        z_bf = [sb.tile([P, NT, PACK], BF16, name="z_bf%d" % q, align_bytes=64) for q in range(CHUNKS)]
+        z_codes = [sb.tile([P, NT], U32, name="z_codes%d" % q, align_bytes=64) for q in range(CHUNKS)]
+        z_scales = [sb.tile([P, NT], U8, name="z_scales%d" % q, align_bytes=64) for q in range(CHUNKS)]
+        out_sb = [sb.tile([P, MT, CHUNK], F32, name="out_sb%d" % i) for i in range(CHUNKS)]
+
+        z_ps = [ps.tile([P, PACK, NT], F32, name="z_ps%d" % i) for i in range(2)]
+        y_ps = [[ps.tile([P, MT, NT], F32, name="y_ps%d_%d" % (t, i)) for i in range(3)] for t in range(2)]
+
+        out_v = out.rearrange("(mt p) n -> p mt n", p=P)
+        bb_v = bb.rearrange("(p j) m -> p j m", j=PACK)
+        x_v = x.rearrange("(p j) n -> p j n", j=PACK)
+        lower = slice(0, ROWS)
+        upper = slice(ROWS, P)
+
+        nc.sync.dma_start(out=bb_raw[lower], in_=bb_v[:, :, 0:HALF_M])
+        nc.scalar.dma_start(out=bb_raw[upper], in_=bb_v[:, :, HALF_M:M])
+        nc.sync.dma_start(out=w_raw[:], in_=w.rearrange("(p j) m -> p j m", j=PACK))
+        nc.sync.dma_start(out=a_raw[:], in_=a.rearrange("(p j) r -> p j r", j=PACK))
+        for q in range(CHUNKS):
+            nc.sync.dma_start(out=x_raw[q][:], in_=x_v[:, :, q * CHUNK:(q + 1) * CHUNK])
+
+        nc.vector.memset(wb_mx[:, 0, W_SCALES:BB_CODES].bitcast(I32), 0)
+        nc.vector.memset(wb_mx[:, 0, BB_SCALES:WB_BYTES].bitcast(I32), 0)
+        nc.vector.memset(a_codes[:], 0)
+        nc.vector.memset(a_scales[:], 127)
+        for q in range(CHUNKS):
+            nc.vector.memset(x_mx[q][:, 0:2, X_SCALES:X_BYTES].bitcast(I32), 0)
+
+        def prepare_weights():
+            interleave(bb_bf, bb_raw, BB_SPLIT)
+            quantize(
+                wb_mx[:, 0, BB_CODES:BB_SCALES],
+                wb_mx[:, 0, BB_SCALES:WB_BYTES],
+                bb_bf[:].rearrange("p m j -> p (m j)"),
+            )
+            interleave(w_bf, w_raw, W_SPLIT)
+            quantize(
+                wb_mx[:, 0, W_CODES:W_SCALES],
+                wb_mx[:, 0, W_SCALES:BB_CODES],
+                w_bf[:].rearrange("p m j -> p (m j)"),
+            )
+            nc.scalar.dma_start(out=wb_mx[upper, 1, :].bitcast(I32), in_=wb_mx[lower, 0, :].bitcast(I32))
+            nc.scalar.dma_start(out=wb_mx[lower, 1, :].bitcast(I32), in_=wb_mx[upper, 0, :].bitcast(I32))
+
+        def prepare_a():
+            src = a_raw[:].rearrange("p j (s i) -> p i s j", i=PACK)
+            nc.vector.tensor_copy(out=a_bf[:, :, 0:A_SPLIT, :], in_=src[:, :, 0:A_SPLIT, :])
+            nc.scalar.copy(out=a_bf[:, :, A_SPLIT:ROWS, :], in_=src[:, :, A_SPLIT:ROWS, :])
+            for i in range(PACK):
+                cols = slice((2 * i + 1) * ROWS, (2 * i + 2) * ROWS)
+                quantize(a_codes[:, cols], a_scales[:, cols], a_bf[:, i].rearrange("p s j -> p (s j)"))
+
+        def quantize_x(q):
+            interleave(x_bf[q], x_raw[q], CHUNK)
+            for t in range(2):
+                quantize(
+                    x_mx[q][:, t, 0:X_SCALES],
+                    x_mx[q][:, t, X_SCALES:X_BYTES],
+                    x_bf[q][:, t * NT:(t + 1) * NT, :].rearrange("p n j -> p (n j)"),
+                )
+
+        def swap_x(q):
+            nc.scalar.dma_start(out=x_mx[q][lower, 2, :].bitcast(I32), in_=x_mx[q][upper, 0, :].bitcast(I32))
+            nc.scalar.dma_start(out=x_mx[q][upper, 2, :].bitcast(I32), in_=x_mx[q][lower, 1, :].bitcast(I32))
+
+        def z_product(q):
+            for i in range(PACK):
+                for t in range(2):
+                    win = slice((2 * i + 1 - t) * ROWS, (2 * i + 3 - t) * ROWS)
+                    nc.tensor.matmul_mx(
+                        out=z_ps[q % 2][:, i, :],
+                        lhsT=a_codes[:, win].bitcast(FP8X4),
+                        lhsT_scale=a_scales[:, win],
+                        rhs=x_mx[q][:, t, 0:X_SCALES].bitcast(FP8X4),
+                        rhs_scale=x_mx[q][:, t, X_SCALES:X_BYTES],
+                        start=(t == 0),
+                        stop=(t == 1),
+                    )
+
+        def z_round(q):
+            nc.scalar.copy(out=z_bf[q][:], in_=z_ps[q % 2][:].rearrange("p i n -> p n i"))
+
+        def quantize_z(q):
+            quantize(z_codes[q][:], z_scales[q][:], z_bf[q][:].rearrange("p n i -> p (n i)"))
+
+        def y_product(q, mts, bank):
+            for mt in mts:
+                for step in range(3):
+                    for t in range(2):
+                        rows = (lower, upper)[t]
+                        if step < 2:
+                            w0 = mt * P
+                            lhs = wb_mx[rows, step, W_CODES + w0 * PACK:W_CODES + (w0 + P) * PACK]
+                            lhs_scale = wb_mx[rows, step, W_SCALES + w0:W_SCALES + w0 + P]
+                            slot = t if step == 0 else 2
+                            rhs = x_mx[q][rows, slot, 0:X_SCALES]
+                            rhs_scale = x_mx[q][rows, slot, X_SCALES:X_BYTES]
+                        else:
+                            slot = 0 if mt // 2 == t else 1
+                            b0 = (mt % 2) * P
+                            lhs = wb_mx[rows, slot, BB_CODES + b0 * PACK:BB_CODES + (b0 + P) * PACK]
+                            lhs_scale = wb_mx[rows, slot, BB_SCALES + b0:BB_SCALES + b0 + P]
+                            rhs = z_codes[q][rows, :]
+                            rhs_scale = z_scales[q][rows, :]
+                        nc.tensor.matmul_mx(
+                            out=y_ps[t][bank][:, mt, :],
+                            lhsT=lhs.bitcast(FP8X4),
+                            lhsT_scale=lhs_scale,
+                            rhs=rhs.bitcast(FP8X4),
+                            rhs_scale=rhs_scale,
+                            start=(step == 0),
+                            stop=(step == 2),
+                        )
+
+        def relu(q, t, mts, bank, on_vector):
+            dst = out_sb[q][:, mts.start:mts.stop, t * NT:(t + 1) * NT]
+            src = y_ps[t][bank][:, mts.start:mts.stop, :]
+            if on_vector:
+                nc.vector.tensor_scalar(out=dst, in0=src, scalar1=0.0, scalar2=None, op0=ALU.max)
+            else:
+                nc.scalar.activation(out=dst, in_=src, func=ACT.Relu)
+
+        def store(q, mts):
+            nc.sync.dma_start(
+                out=out_v[:, mts.start:mts.stop, q * CHUNK:(q + 1) * CHUNK],
+                in_=out_sb[q][:, mts.start:mts.stop, :],
+            )
+
+        every = range(MT)
+        first = range(0, MT // 2)
+        second = range(MT // 2, MT)
+
+        prepare_weights()
+        prepare_a()
+        quantize_x(0)
+        swap_x(0)
+        z_product(0)
+        z_round(0)
+        quantize_x(1)
+        swap_x(1)
+        z_product(1)
+        quantize_z(0)
+        y_product(0, every, 0)
+        z_round(1)
+        quantize_x(2)
+        swap_x(2)
+        z_product(2)
+        quantize_z(1)
+        y_product(1, every, 1)
+        relu(0, 0, every, 0, False)
+        z_round(2)
+        relu(0, 1, every, 0, False)
+        store(0, every)
+        quantize_x(3)
+        swap_x(3)
+        z_product(3)
+        quantize_z(2)
+        y_product(2, every, 2)
+        relu(1, 1, every, 1, True)
+        relu(1, 0, every, 1, False)
+        store(1, every)
+        z_round(3)
+        quantize_z(3)
+        y_product(3, first, 0)
+        y_product(3, second, 1)
+        relu(2, 1, every, 2, True)
+        relu(2, 0, every, 2, False)
+        store(2, every)
+        relu(3, 1, first, 0, True)
+        relu(3, 0, first, 0, False)
+        store(3, first)
+        relu(3, 1, second, 1, True)
+        relu(3, 0, second, 1, False)
+        store(3, second)

@@ -20,36 +20,19 @@ ROWS = 64
 NT = 128
 CHUNK = 2 * NT
 CHUNKS = N // CHUNK
-MT = M // P
 HALF_M = M // 2
-
-W_CODES = 0
-W_SCALES = W_CODES + M * PACK
-BB_CODES = W_SCALES + M
-BB_SCALES = BB_CODES + HALF_M * PACK
-WB_BYTES = BB_SCALES + HALF_M
+W_SCALES = HALF_M * PACK
+W_BYTES = W_SCALES + HALF_M
 X_SCALES = NT * PACK
 X_BYTES = X_SCALES + NT
-
-BB_SPLIT = 176
-A_SPLIT = 44
-W_SPLIT = 336
+SWAPPED = (2, 3)
+VECTOR, SCALAR = 0, 1
 
 
 def tile_rows_lora_relu_kernel(tc, x, w, a, bb, out):
     nc = tc.nc
-
-    def interleave(dst, src, split):
-        cols = src.shape[2]
-        for lo, hi, copy in ((0, split, nc.vector.tensor_copy), (split, cols, nc.scalar.copy)):
-            if hi > lo:
-                copy(
-                    out=dst[:, lo:hi, :].rearrange("p (c i) j -> p c j i", i=4),
-                    in_=src[:, :, lo:hi].rearrange("p j (c i) -> p c j i", i=4),
-                )
-
-    def quantize(codes, scales, grouped):
-        nc.vector.quantize_mx(out=codes.bitcast(FP8X4), scales=scales, in_=grouped)
+    copy = (nc.vector.tensor_copy, nc.scalar.copy)
+    half = (slice(0, ROWS), slice(ROWS, P))
 
     with ExitStack() as ctx:
         sb = ctx.enter_context(tc.tile_pool(name="sb", bufs=1))
@@ -58,70 +41,87 @@ def tile_rows_lora_relu_kernel(tc, x, w, a, bb, out):
 
         bb_raw = sb.tile([P, PACK, HALF_M], F32, name="bb_raw")
         bb_bf = sb.tile([P, HALF_M, PACK], BF16, name="bb_bf", align_bytes=64)
-        wb_mx = sb.tile([P, 2, WB_BYTES], U8, name="wb_mx", align_bytes=64)
+        bb_mx = sb.tile([P, 2, W_BYTES], U8, name="bb_mx", align_bytes=64)
         a_raw = sb.tile([P, PACK, R], F32, name="a_raw")
         a_bf = sb.tile([P, PACK, ROWS, PACK], BF16, name="a_bf", align_bytes=64)
         a_codes = sb.tile([P, (2 * PACK + 1) * ROWS], U32, name="a_codes", align_bytes=64)
         a_scales = sb.tile([P, (2 * PACK + 1) * ROWS], U8, name="a_scales", align_bytes=64)
         w_raw = sb.tile([P, PACK, M], F32, name="w_raw")
-        w_bf = sb.tile([P, M, PACK], BF16, name="w_bf", align_bytes=64)
+        w_bf = [sb.tile([P, HALF_M, PACK], BF16, name="w_bf%d" % h, align_bytes=64) for h in range(2)]
+        w_mx = sb.tile([P, 2, 2 * W_BYTES], U8, name="w_mx", align_bytes=64)
         x_raw = [sb.tile([P, PACK, CHUNK], F32, name="x_raw%d" % q) for q in range(CHUNKS)]
         x_bf = [sb.tile([P, CHUNK, PACK], BF16, name="x_bf%d" % q, align_bytes=64) for q in range(CHUNKS)]
         x_mx = [sb.tile([P, 3, X_BYTES], U8, name="x_mx%d" % q, align_bytes=64) for q in range(CHUNKS)]
         z_bf = [sb.tile([P, NT, PACK], BF16, name="z_bf%d" % q, align_bytes=64) for q in range(CHUNKS)]
         z_codes = [sb.tile([P, NT], U32, name="z_codes%d" % q, align_bytes=64) for q in range(CHUNKS)]
         z_scales = [sb.tile([P, NT], U8, name="z_scales%d" % q, align_bytes=64) for q in range(CHUNKS)]
-        out_sb = [sb.tile([P, MT, CHUNK], F32, name="out_sb%d" % i) for i in range(CHUNKS)]
+        main_sb = [[sb.tile([P, 2, CHUNK], F32, name="main_sb%d_%d" % (q, h)) for h in range(2)] for q in range(CHUNKS)]
+        sum_sb = [[sb.tile([P, 2, CHUNK], F32, name="sum_sb%d_%d" % (q, h)) for h in range(2)] for q in range(CHUNKS)]
+        out_sb = [[sb.tile([P, 2, CHUNK], F32, name="out_sb%d_%d" % (q, h)) for h in range(2)] for q in range(CHUNKS)]
 
-        z_ps = [ps.tile([P, PACK, NT], F32, name="z_ps%d" % i) for i in range(2)]
-        y_ps = [[ps.tile([P, MT, NT], F32, name="y_ps%d_%d" % (t, i)) for i in range(3)] for t in range(2)]
+        z_ps = [ps.tile([P, PACK, NT], F32, name="z_ps%d" % i) for i in range(1)]
+        main_ps = [ps.tile([P, 2, CHUNK], F32, name="main_ps%d" % i) for i in range(1)]
+        row_ps = [[ps.tile([P, 2, NT], F32, name="row_ps%d_%d" % (t, i)) for i in range(3)] for t in range(2)]
 
         out_v = out.rearrange("(mt p) n -> p mt n", p=P)
         bb_v = bb.rearrange("(p j) m -> p j m", j=PACK)
         x_v = x.rearrange("(p j) n -> p j n", j=PACK)
-        lower = slice(0, ROWS)
-        upper = slice(ROWS, P)
+        w_v = w.rearrange("(p j) m -> p j m", j=PACK)
 
-        nc.sync.dma_start(out=bb_raw[lower], in_=bb_v[:, :, 0:HALF_M])
-        nc.scalar.dma_start(out=bb_raw[upper], in_=bb_v[:, :, HALF_M:M])
-        nc.sync.dma_start(out=w_raw[:], in_=w.rearrange("(p j) m -> p j m", j=PACK))
-        nc.sync.dma_start(out=a_raw[:], in_=a.rearrange("(p j) r -> p j r", j=PACK))
-        for q in range(CHUNKS):
-            nc.sync.dma_start(out=x_raw[q][:], in_=x_v[:, :, q * CHUNK:(q + 1) * CHUNK])
+        def load_a(queue):
+            queue.dma_start(out=a_raw[:], in_=a.rearrange("(p j) r -> p j r", j=PACK))
 
-        nc.vector.memset(wb_mx[:, 0, W_SCALES:BB_CODES].bitcast(I32), 0)
-        nc.vector.memset(wb_mx[:, 0, BB_SCALES:WB_BYTES].bitcast(I32), 0)
-        nc.vector.memset(a_codes[:], 0)
-        nc.vector.memset(a_scales[:], 127)
-        for q in range(CHUNKS):
-            nc.vector.memset(x_mx[q][:, 0:2, X_SCALES:X_BYTES].bitcast(I32), 0)
+        def load_bb(queue, t):
+            queue.dma_start(out=bb_raw[half[t]], in_=bb_v[:, :, t * HALF_M:(t + 1) * HALF_M])
 
-        def prepare_weights():
-            interleave(bb_bf, bb_raw, BB_SPLIT)
-            quantize(
-                wb_mx[:, 0, BB_CODES:BB_SCALES],
-                wb_mx[:, 0, BB_SCALES:WB_BYTES],
-                bb_bf[:].rearrange("p m j -> p (m j)"),
+        def load_w(queue, lo, hi):
+            queue.dma_start(out=w_raw[:], in_=w_v[:, :, lo:hi])
+
+        def load_x(queue, q):
+            queue.dma_start(out=x_raw[q][:], in_=x_v[:, :, q * CHUNK:(q + 1) * CHUNK])
+
+        def clear():
+            nc.vector.memset(a_codes[:], 0)
+            nc.vector.memset(a_scales[:], 127)
+            nc.vector.memset(bb_mx[:, 0, W_SCALES:W_BYTES].bitcast(I32), 0)
+            for h in range(2):
+                nc.vector.memset(w_mx[:, 0, h * W_BYTES + W_SCALES:(h + 1) * W_BYTES].bitcast(I32), 0)
+            for q in SWAPPED:
+                nc.vector.memset(x_mx[q][:, 0:2, X_SCALES:X_BYTES].bitcast(I32), 0)
+
+        def interleave(engine, dst, src, lo, hi):
+            copy[engine](
+                out=dst[:, lo:hi, :].rearrange("p (c i) j -> p c j i", i=4),
+                in_=src[:, :, lo:hi].rearrange("p j (c i) -> p c j i", i=4),
             )
-            interleave(w_bf, w_raw, W_SPLIT)
-            quantize(
-                wb_mx[:, 0, W_CODES:W_SCALES],
-                wb_mx[:, 0, W_SCALES:BB_CODES],
-                w_bf[:].rearrange("p m j -> p (m j)"),
-            )
-            nc.scalar.dma_start(out=wb_mx[upper, 1, :].bitcast(I32), in_=wb_mx[lower, 0, :].bitcast(I32))
-            nc.scalar.dma_start(out=wb_mx[lower, 1, :].bitcast(I32), in_=wb_mx[upper, 0, :].bitcast(I32))
 
-        def prepare_a():
+        def round_w(engine, h, lo, hi):
+            interleave(engine, w_bf[h], w_raw[:, :, h * HALF_M:(h + 1) * HALF_M], lo, hi)
+
+        def round_a(engine, lo, hi):
             src = a_raw[:].rearrange("p j (s i) -> p i s j", i=PACK)
-            nc.vector.tensor_copy(out=a_bf[:, :, 0:A_SPLIT, :], in_=src[:, :, 0:A_SPLIT, :])
-            nc.scalar.copy(out=a_bf[:, :, A_SPLIT:ROWS, :], in_=src[:, :, A_SPLIT:ROWS, :])
+            copy[engine](out=a_bf[:, :, lo:hi, :], in_=src[:, :, lo:hi, :])
+
+        def quantize(codes, scales, grouped):
+            nc.vector.quantize_mx(out=codes.bitcast(FP8X4), scales=scales, in_=grouped)
+
+        def quantize_a():
             for i in range(PACK):
                 cols = slice((2 * i + 1) * ROWS, (2 * i + 2) * ROWS)
                 quantize(a_codes[:, cols], a_scales[:, cols], a_bf[:, i].rearrange("p s j -> p (s j)"))
 
+        def quantize_bb():
+            quantize(bb_mx[:, 0, 0:W_SCALES], bb_mx[:, 0, W_SCALES:W_BYTES], bb_bf[:].rearrange("p m j -> p (m j)"))
+
+        def quantize_w(h):
+            b0 = h * W_BYTES
+            quantize(
+                w_mx[:, 0, b0:b0 + W_SCALES],
+                w_mx[:, 0, b0 + W_SCALES:b0 + W_BYTES],
+                w_bf[h][:].rearrange("p m j -> p (m j)"),
+            )
+
         def quantize_x(q):
-            interleave(x_bf[q], x_raw[q], CHUNK)
             for t in range(2):
                 quantize(
                     x_mx[q][:, t, 0:X_SCALES],
@@ -129,16 +129,31 @@ def tile_rows_lora_relu_kernel(tc, x, w, a, bb, out):
                     x_bf[q][:, t * NT:(t + 1) * NT, :].rearrange("p n j -> p (n j)"),
                 )
 
-        def swap_x(q):
-            nc.scalar.dma_start(out=x_mx[q][lower, 2, :].bitcast(I32), in_=x_mx[q][upper, 0, :].bitcast(I32))
-            nc.scalar.dma_start(out=x_mx[q][upper, 2, :].bitcast(I32), in_=x_mx[q][lower, 1, :].bitcast(I32))
+        def quantize_z(q):
+            quantize(z_codes[q][:], z_scales[q][:], z_bf[q][:].rearrange("p n i -> p (n i)"))
 
-        def z_product(q):
+        def send(queue, src, dst, t):
+            queue.dma_start(out=dst[half[t]].bitcast(I32), in_=src[half[1 - t]].bitcast(I32))
+
+        def warm_up():
+            for i in range(PACK):
+                win = slice((2 * i + 1) * ROWS, (2 * i + 3) * ROWS)
+                nc.tensor.matmul_mx(
+                    out=main_ps[0][:, i // 2, (i % 2) * NT:(i % 2 + 1) * NT],
+                    lhsT=a_codes[:, win].bitcast(FP8X4),
+                    lhsT_scale=a_scales[:, win],
+                    rhs=a_codes[:, win].bitcast(FP8X4),
+                    rhs_scale=a_scales[:, win],
+                    start=True,
+                    stop=True,
+                )
+
+        def z_product(q, bank):
             for i in range(PACK):
                 for t in range(2):
                     win = slice((2 * i + 1 - t) * ROWS, (2 * i + 3 - t) * ROWS)
                     nc.tensor.matmul_mx(
-                        out=z_ps[q % 2][:, i, :],
+                        out=z_ps[bank][:, i, :],
                         lhsT=a_codes[:, win].bitcast(FP8X4),
                         lhsT_scale=a_scales[:, win],
                         rhs=x_mx[q][:, t, 0:X_SCALES].bitcast(FP8X4),
@@ -147,98 +162,156 @@ def tile_rows_lora_relu_kernel(tc, x, w, a, bb, out):
                         stop=(t == 1),
                     )
 
-        def z_round(q):
-            nc.scalar.copy(out=z_bf[q][:], in_=z_ps[q % 2][:].rearrange("p i n -> p n i"))
+        def z_round(engine, q, bank):
+            copy[engine](out=z_bf[q][:], in_=z_ps[bank][:].rearrange("p i n -> p n i"))
 
-        def quantize_z(q):
-            quantize(z_codes[q][:], z_scales[q][:], z_bf[q][:].rearrange("p n i -> p (n i)"))
+        def main_product(q, h, bank):
+            for s in range(2):
+                c0 = h * W_BYTES + s * P * PACK
+                s0 = h * W_BYTES + W_SCALES + s * P
+                for t in range(2):
+                    nc.tensor.matmul_mx(
+                        out=main_ps[bank][:, s, t * NT:(t + 1) * NT],
+                        lhsT=w_mx[:, 0, c0:c0 + P * PACK].bitcast(FP8X4),
+                        lhsT_scale=w_mx[:, 0, s0:s0 + P],
+                        rhs=x_mx[q][:, t, 0:X_SCALES].bitcast(FP8X4),
+                        rhs_scale=x_mx[q][:, t, X_SCALES:X_BYTES],
+                        start=True,
+                        stop=True,
+                    )
 
-        def y_product(q, mts, bank):
-            for mt in mts:
-                for step in range(3):
+        def y_product(q, h, bank, first):
+            for s in range(2):
+                for step in range(first, 3):
                     for t in range(2):
-                        rows = (lower, upper)[t]
+                        rows = half[t]
                         if step < 2:
-                            w0 = mt * P
-                            lhs = wb_mx[rows, step, W_CODES + w0 * PACK:W_CODES + (w0 + P) * PACK]
-                            lhs_scale = wb_mx[rows, step, W_SCALES + w0:W_SCALES + w0 + P]
+                            held = w_mx[rows, step, h * W_BYTES:(h + 1) * W_BYTES]
                             slot = t if step == 0 else 2
                             rhs = x_mx[q][rows, slot, 0:X_SCALES]
                             rhs_scale = x_mx[q][rows, slot, X_SCALES:X_BYTES]
                         else:
-                            slot = 0 if mt // 2 == t else 1
-                            b0 = (mt % 2) * P
-                            lhs = wb_mx[rows, slot, BB_CODES + b0 * PACK:BB_CODES + (b0 + P) * PACK]
-                            lhs_scale = wb_mx[rows, slot, BB_SCALES + b0:BB_SCALES + b0 + P]
+                            held = bb_mx[rows, 0 if h == t else 1]
                             rhs = z_codes[q][rows, :]
                             rhs_scale = z_scales[q][rows, :]
                         nc.tensor.matmul_mx(
-                            out=y_ps[t][bank][:, mt, :],
-                            lhsT=lhs.bitcast(FP8X4),
-                            lhsT_scale=lhs_scale,
+                            out=row_ps[t][bank][:, s, :],
+                            lhsT=held[:, s * P * PACK:(s + 1) * P * PACK].bitcast(FP8X4),
+                            lhsT_scale=held[:, W_SCALES + s * P:W_SCALES + (s + 1) * P],
                             rhs=rhs.bitcast(FP8X4),
                             rhs_scale=rhs_scale,
-                            start=(step == 0),
+                            start=(step == first),
                             stop=(step == 2),
                         )
 
-        def relu(q, t, mts, bank, on_vector):
-            dst = out_sb[q][:, mts.start:mts.stop, t * NT:(t + 1) * NT]
-            src = y_ps[t][bank][:, mts.start:mts.stop, :]
-            if on_vector:
+        def main_copy(engine, q, h, bank):
+            copy[engine](out=main_sb[q][h][:], in_=main_ps[bank][:])
+
+        def add(q, h, t, bank):
+            cols = slice(t * NT, (t + 1) * NT)
+            nc.vector.tensor_tensor(
+                out=sum_sb[q][h][:, :, cols], in0=row_ps[t][bank][:], in1=main_sb[q][h][:, :, cols], op=ALU.add
+            )
+
+        def relu(engine, dst, src):
+            if engine == VECTOR:
                 nc.vector.tensor_scalar(out=dst, in0=src, scalar1=0.0, scalar2=None, op0=ALU.max)
             else:
                 nc.scalar.activation(out=dst, in_=src, func=ACT.Relu)
 
-        def store(q, mts):
-            nc.sync.dma_start(
-                out=out_v[:, mts.start:mts.stop, q * CHUNK:(q + 1) * CHUNK],
-                in_=out_sb[q][:, mts.start:mts.stop, :],
-            )
+        def store(queue, q, h):
+            queue.dma_start(out=out_v[:, 2 * h:2 * h + 2, q * CHUNK:(q + 1) * CHUNK], in_=out_sb[q][h][:])
 
-        every = range(MT)
-        first = range(0, MT // 2)
-        second = range(MT // 2, MT)
-
-        prepare_weights()
-        prepare_a()
+        load_bb(nc.scalar, 1)
+        load_bb(nc.sync, 0)
+        load_a(nc.sync)
+        interleave(SCALAR, bb_bf, bb_raw, 0, 256)
+        load_x(nc.sync, 0)
+        clear()
+        round_a(VECTOR, 0, 64)
+        load_w(nc.sync, 0, M)
+        quantize_bb()
+        quantize_a()
+        interleave(VECTOR, x_bf[0], x_raw[0], 0, 256)
         quantize_x(0)
-        swap_x(0)
-        z_product(0)
-        z_round(0)
+        load_x(nc.sync, 1)
+        round_w(SCALAR, 1, 64, 256)
+        load_x(nc.sync, 2)
+        send(nc.scalar, bb_mx[:, 0, :], bb_mx[:, 1, :], 1)
+        round_w(VECTOR, 0, 0, 256)
+        quantize_w(0)
+        interleave(VECTOR, x_bf[1], x_raw[1], 0, 160)
+        z_product(0, 0)
+        send(nc.sync, bb_mx[:, 0, :], bb_mx[:, 1, :], 0)
+        round_w(VECTOR, 1, 0, 64)
+        interleave(SCALAR, x_bf[1], x_raw[1], 160, 256)
+        load_x(nc.sync, 3)
+        main_product(0, 0, 0)
         quantize_x(1)
-        swap_x(1)
-        z_product(1)
+        quantize_w(1)
+        z_round(SCALAR, 0, 0)
+        main_copy(SCALAR, 0, 0, 0)
         quantize_z(0)
-        y_product(0, every, 0)
-        z_round(1)
+        interleave(VECTOR, x_bf[2], x_raw[2], 0, 160)
+        interleave(SCALAR, x_bf[2], x_raw[2], 160, 256)
+        z_product(1, 0)
+        send(nc.sync, w_mx[:, 0, :], w_mx[:, 1, :], 0)
+        main_product(0, 1, 0)
+        z_round(SCALAR, 1, 0)
+        y_product(0, 0, 0, 2)
         quantize_x(2)
-        swap_x(2)
-        z_product(2)
+        y_product(0, 1, 1, 2)
+        z_product(2, 0)
+        add(0, 0, 1, 0)
+        send(nc.sync, w_mx[:, 0, :], w_mx[:, 1, :], 1)
         quantize_z(1)
-        y_product(1, every, 1)
-        relu(0, 0, every, 0, False)
-        z_round(2)
-        relu(0, 1, every, 0, False)
-        store(0, every)
+        interleave(VECTOR, x_bf[3], x_raw[3], 0, 160)
+        main_copy(SCALAR, 0, 1, 0)
+        interleave(SCALAR, x_bf[3], x_raw[3], 160, 256)
+        add(0, 0, 0, 0)
         quantize_x(3)
-        swap_x(3)
-        z_product(3)
+        send(nc.sync, x_mx[2][:, 1, :], x_mx[2][:, 2, :], 1)
+        z_round(SCALAR, 2, 0)
+        main_product(1, 0, 0)
+        send(nc.sync, x_mx[2][:, 0, :], x_mx[2][:, 2, :], 0)
+        main_copy(SCALAR, 1, 0, 0)
+        send(nc.sync, x_mx[3][:, 0, :], x_mx[3][:, 2, :], 0)
+        add(0, 1, 0, 1)
+        send(nc.sync, x_mx[3][:, 1, :], x_mx[3][:, 2, :], 1)
+        relu(SCALAR, out_sb[0][0][:], sum_sb[0][0][:])
+        add(0, 1, 1, 1)
+        y_product(1, 0, 2, 2)
         quantize_z(2)
-        y_product(2, every, 2)
-        relu(1, 1, every, 1, True)
-        relu(1, 0, every, 1, False)
-        store(1, every)
-        z_round(3)
+        relu(VECTOR, out_sb[0][1][:], sum_sb[0][1][:])
+        y_product(1, 1, 0, 2)
+        add(1, 0, 1, 2)
+        z_product(3, 0)
+        add(1, 0, 0, 2)
+        relu(VECTOR, out_sb[1][0][:], sum_sb[1][0][:])
+        z_round(SCALAR, 3, 0)
+        main_product(1, 1, 0)
+        store(nc.sync, 0, 1)
+        y_product(2, 0, 1, 0)
+        main_copy(SCALAR, 1, 1, 0)
+        store(nc.sync, 0, 0)
         quantize_z(3)
-        y_product(3, first, 0)
-        y_product(3, second, 1)
-        relu(2, 1, every, 2, True)
-        relu(2, 0, every, 2, False)
-        store(2, every)
-        relu(3, 1, first, 0, True)
-        relu(3, 0, first, 0, False)
-        store(3, first)
-        relu(3, 1, second, 1, True)
-        relu(3, 0, second, 1, False)
-        store(3, second)
+        store(nc.sync, 1, 0)
+        relu(SCALAR, out_sb[2][0][:, :, 1 * NT:2 * NT], row_ps[1][1][:])
+        relu(SCALAR, out_sb[2][0][:, :, 0 * NT:1 * NT], row_ps[0][1][:])
+        add(1, 1, 0, 0)
+        add(1, 1, 1, 0)
+        y_product(2, 1, 2, 0)
+        relu(SCALAR, out_sb[2][1][:, :, 0 * NT:1 * NT], row_ps[0][2][:])
+        relu(VECTOR, out_sb[1][1][:], sum_sb[1][1][:])
+        store(nc.sync, 2, 0)
+        y_product(3, 0, 0, 0)
+        relu(VECTOR, out_sb[3][0][:, :, 1 * NT:2 * NT], row_ps[1][0][:])
+        y_product(3, 1, 1, 0)
+        store(nc.scalar, 1, 1)
+        relu(SCALAR, out_sb[2][1][:, :, 1 * NT:2 * NT], row_ps[1][2][:])
+        relu(SCALAR, out_sb[3][1][:, :, 1 * NT:2 * NT], row_ps[1][1][:])
+        store(nc.sync, 2, 1)
+        relu(VECTOR, out_sb[3][0][:, :, 0 * NT:1 * NT], row_ps[0][0][:])
+        store(nc.sync, 3, 0)
+        relu(VECTOR, out_sb[3][1][:, :, 0 * NT:1 * NT], row_ps[0][1][:])
+        store(nc.sync, 3, 1)

@@ -21,18 +21,27 @@ NT = 128
 CHUNK = 2 * NT
 CHUNKS = N // CHUNK
 HALF_M = M // 2
+
 W_SCALES = HALF_M * PACK
 W_BYTES = W_SCALES + HALF_M
 X_SCALES = NT * PACK
 X_BYTES = X_SCALES + NT
-SWAPPED = (2, 3)
+
+HELD, SENT = 0, 1
+X_SENT = 2
+OWN_K, OTHER_K, RANK = 0, 1, 2
+ROW_BANKS = 3
 VECTOR, SCALAR = 0, 1
+
+W1_ON_VECTOR = 64
+X1_ON_VECTOR = 176
+X2_ON_VECTOR = 192
 
 
 def tile_rows_lora_relu_kernel(tc, x, w, a, bb, out):
     nc = tc.nc
     copy = (nc.vector.tensor_copy, nc.scalar.copy)
-    half = (slice(0, ROWS), slice(ROWS, P))
+    tile_rows = (slice(0, ROWS), slice(ROWS, P))
 
     with ExitStack() as ctx:
         sb = ctx.enter_context(tc.tile_pool(name="sb", bufs=1))
@@ -55,27 +64,26 @@ def tile_rows_lora_relu_kernel(tc, x, w, a, bb, out):
         z_bf = [sb.tile([P, NT, PACK], BF16, name="z_bf%d" % q, align_bytes=64) for q in range(CHUNKS)]
         z_codes = [sb.tile([P, NT], U32, name="z_codes%d" % q, align_bytes=64) for q in range(CHUNKS)]
         z_scales = [sb.tile([P, NT], U8, name="z_scales%d" % q, align_bytes=64) for q in range(CHUNKS)]
-        main_sb = [[sb.tile([P, 2, CHUNK], F32, name="main_sb%d_%d" % (q, h)) for h in range(2)] for q in range(CHUNKS)]
-        sum_sb = [[sb.tile([P, 2, CHUNK], F32, name="sum_sb%d_%d" % (q, h)) for h in range(2)] for q in range(CHUNKS)]
+        main_sb = [sb.tile([P, 2, CHUNK], F32, name="main_sb%d" % h) for h in range(2)]
+        sum_sb = [sb.tile([P, 2, CHUNK], F32, name="sum_sb%d" % h) for h in range(2)]
         out_sb = [[sb.tile([P, 2, CHUNK], F32, name="out_sb%d_%d" % (q, h)) for h in range(2)] for q in range(CHUNKS)]
 
-        z_ps = [ps.tile([P, PACK, NT], F32, name="z_ps%d" % i) for i in range(1)]
-        main_ps = [ps.tile([P, 2, CHUNK], F32, name="main_ps%d" % i) for i in range(1)]
-        row_ps = [[ps.tile([P, 2, NT], F32, name="row_ps%d_%d" % (t, i)) for i in range(3)] for t in range(2)]
+        z_ps = ps.tile([P, PACK, NT], F32, name="z_ps")
+        main_ps = ps.tile([P, 2, CHUNK], F32, name="main_ps")
+        row_ps = [[ps.tile([P, 2, NT], F32, name="row_ps%d_%d" % (t, b)) for b in range(ROW_BANKS)] for t in range(2)]
 
         out_v = out.rearrange("(mt p) n -> p mt n", p=P)
         bb_v = bb.rearrange("(p j) m -> p j m", j=PACK)
         x_v = x.rearrange("(p j) n -> p j n", j=PACK)
-        w_v = w.rearrange("(p j) m -> p j m", j=PACK)
 
-        def load_a(queue):
-            queue.dma_start(out=a_raw[:], in_=a.rearrange("(p j) r -> p j r", j=PACK))
+        def load_a():
+            nc.sync.dma_start(out=a_raw[:], in_=a.rearrange("(p j) r -> p j r", j=PACK))
+
+        def load_w():
+            nc.sync.dma_start(out=w_raw[:], in_=w.rearrange("(p j) m -> p j m", j=PACK))
 
         def load_bb(queue, t):
-            queue.dma_start(out=bb_raw[half[t]], in_=bb_v[:, :, t * HALF_M:(t + 1) * HALF_M])
-
-        def load_w(queue, lo, hi):
-            queue.dma_start(out=w_raw[:], in_=w_v[:, :, lo:hi])
+            queue.dma_start(out=bb_raw[tile_rows[t]], in_=bb_v[:, :, t * HALF_M:(t + 1) * HALF_M])
 
         def load_x(queue, q):
             queue.dma_start(out=x_raw[q][:], in_=x_v[:, :, q * CHUNK:(q + 1) * CHUNK])
@@ -83,11 +91,11 @@ def tile_rows_lora_relu_kernel(tc, x, w, a, bb, out):
         def clear():
             nc.vector.memset(a_codes[:], 0)
             nc.vector.memset(a_scales[:], 127)
-            nc.vector.memset(bb_mx[:, 0, W_SCALES:W_BYTES].bitcast(I32), 0)
+            nc.vector.memset(bb_mx[:, HELD, W_SCALES:W_BYTES].bitcast(I32), 0)
             for h in range(2):
-                nc.vector.memset(w_mx[:, 0, h * W_BYTES + W_SCALES:(h + 1) * W_BYTES].bitcast(I32), 0)
-            for q in SWAPPED:
-                nc.vector.memset(x_mx[q][:, 0:2, X_SCALES:X_BYTES].bitcast(I32), 0)
+                nc.vector.memset(w_mx[:, HELD, h * W_BYTES + W_SCALES:(h + 1) * W_BYTES].bitcast(I32), 0)
+            for q in range(1, CHUNKS):
+                nc.vector.memset(x_mx[q][:, 0:X_SENT, X_SCALES:X_BYTES].bitcast(I32), 0)
 
         def interleave(engine, dst, src, lo, hi):
             copy[engine](
@@ -95,31 +103,39 @@ def tile_rows_lora_relu_kernel(tc, x, w, a, bb, out):
                 in_=src[:, :, lo:hi].rearrange("p j (c i) -> p c j i", i=4),
             )
 
+        def round_bb():
+            interleave(VECTOR, bb_bf, bb_raw, 0, HALF_M)
+
         def round_w(engine, h, lo, hi):
             interleave(engine, w_bf[h], w_raw[:, :, h * HALF_M:(h + 1) * HALF_M], lo, hi)
 
-        def round_a(engine, lo, hi):
-            src = a_raw[:].rearrange("p j (s i) -> p i s j", i=PACK)
-            copy[engine](out=a_bf[:, :, lo:hi, :], in_=src[:, :, lo:hi, :])
+        def round_x(engine, q, lo, hi):
+            interleave(engine, x_bf[q], x_raw[q], lo, hi)
+
+        def round_a():
+            nc.vector.tensor_copy(
+                out=a_bf[:].rearrange("p i s j -> p s j i"),
+                in_=a_raw[:].rearrange("p j (s i) -> p s j i", i=PACK),
+            )
 
         def quantize(codes, scales, grouped):
             nc.vector.quantize_mx(out=codes.bitcast(FP8X4), scales=scales, in_=grouped)
 
         def quantize_a():
             for i in range(PACK):
-                cols = slice((2 * i + 1) * ROWS, (2 * i + 2) * ROWS)
-                quantize(a_codes[:, cols], a_scales[:, cols], a_bf[:, i].rearrange("p s j -> p (s j)"))
+                strip = slice((2 * i + 1) * ROWS, (2 * i + 2) * ROWS)
+                quantize(a_codes[:, strip], a_scales[:, strip], a_bf[:, i].rearrange("p s j -> p (s j)"))
 
         def quantize_bb():
-            quantize(bb_mx[:, 0, 0:W_SCALES], bb_mx[:, 0, W_SCALES:W_BYTES], bb_bf[:].rearrange("p m j -> p (m j)"))
+            held = bb_mx[:, HELD]
+            quantize(held[:, 0:W_SCALES], held[:, W_SCALES:W_BYTES], bb_bf[:].rearrange("p m j -> p (m j)"))
+
+        def w_half(place, h):
+            return w_mx[:, place, h * W_BYTES:(h + 1) * W_BYTES]
 
         def quantize_w(h):
-            b0 = h * W_BYTES
-            quantize(
-                w_mx[:, 0, b0:b0 + W_SCALES],
-                w_mx[:, 0, b0 + W_SCALES:b0 + W_BYTES],
-                w_bf[h][:].rearrange("p m j -> p (m j)"),
-            )
+            held = w_half(HELD, h)
+            quantize(held[:, 0:W_SCALES], held[:, W_SCALES:W_BYTES], w_bf[h][:].rearrange("p m j -> p (m j)"))
 
         def quantize_x(q):
             for t in range(2):
@@ -133,84 +149,91 @@ def tile_rows_lora_relu_kernel(tc, x, w, a, bb, out):
             quantize(z_codes[q][:], z_scales[q][:], z_bf[q][:].rearrange("p n i -> p (n i)"))
 
         def send(queue, src, dst, t):
-            queue.dma_start(out=dst[half[t]].bitcast(I32), in_=src[half[1 - t]].bitcast(I32))
+            queue.dma_start(out=dst[tile_rows[t]].bitcast(I32), in_=src[tile_rows[1 - t]].bitcast(I32))
 
-        def warm_up():
-            for i in range(PACK):
-                win = slice((2 * i + 1) * ROWS, (2 * i + 3) * ROWS)
-                nc.tensor.matmul_mx(
-                    out=main_ps[0][:, i // 2, (i % 2) * NT:(i % 2 + 1) * NT],
-                    lhsT=a_codes[:, win].bitcast(FP8X4),
-                    lhsT_scale=a_scales[:, win],
-                    rhs=a_codes[:, win].bitcast(FP8X4),
-                    rhs_scale=a_scales[:, win],
-                    start=True,
-                    stop=True,
-                )
+        def send_bb(queue, t):
+            send(queue, bb_mx[:, HELD, :], bb_mx[:, SENT, :], t)
 
-        def z_product(q, bank):
+        def send_w(queue, h, t):
+            send(queue, w_half(HELD, h), w_half(SENT, h), t)
+
+        def send_x(queue, q, t):
+            send(queue, x_mx[q][:, t, :], x_mx[q][:, X_SENT, :], t)
+
+        def z_product(q):
             for i in range(PACK):
                 for t in range(2):
-                    win = slice((2 * i + 1 - t) * ROWS, (2 * i + 3 - t) * ROWS)
+                    window = slice((2 * i + 1 - t) * ROWS, (2 * i + 3 - t) * ROWS)
                     nc.tensor.matmul_mx(
-                        out=z_ps[bank][:, i, :],
-                        lhsT=a_codes[:, win].bitcast(FP8X4),
-                        lhsT_scale=a_scales[:, win],
+                        out=z_ps[:, i, :],
+                        lhsT=a_codes[:, window].bitcast(FP8X4),
+                        lhsT_scale=a_scales[:, window],
                         rhs=x_mx[q][:, t, 0:X_SCALES].bitcast(FP8X4),
                         rhs_scale=x_mx[q][:, t, X_SCALES:X_BYTES],
                         start=(t == 0),
                         stop=(t == 1),
                     )
 
-        def z_round(engine, q, bank):
-            copy[engine](out=z_bf[q][:], in_=z_ps[bank][:].rearrange("p i n -> p n i"))
+        def round_z(engine, q):
+            copy[engine](out=z_bf[q][:], in_=z_ps[:].rearrange("p i n -> p n i"))
 
-        def main_product(q, h, bank):
+        def main_product(h):
+            held = w_half(HELD, h)
             for s in range(2):
-                c0 = h * W_BYTES + s * P * PACK
-                s0 = h * W_BYTES + W_SCALES + s * P
                 for t in range(2):
                     nc.tensor.matmul_mx(
-                        out=main_ps[bank][:, s, t * NT:(t + 1) * NT],
-                        lhsT=w_mx[:, 0, c0:c0 + P * PACK].bitcast(FP8X4),
-                        lhsT_scale=w_mx[:, 0, s0:s0 + P],
-                        rhs=x_mx[q][:, t, 0:X_SCALES].bitcast(FP8X4),
-                        rhs_scale=x_mx[q][:, t, X_SCALES:X_BYTES],
+                        out=main_ps[:, s, t * NT:(t + 1) * NT],
+                        lhsT=held[:, s * P * PACK:(s + 1) * P * PACK].bitcast(FP8X4),
+                        lhsT_scale=held[:, W_SCALES + s * P:W_SCALES + (s + 1) * P],
+                        rhs=x_mx[0][:, t, 0:X_SCALES].bitcast(FP8X4),
+                        rhs_scale=x_mx[0][:, t, X_SCALES:X_BYTES],
                         start=True,
                         stop=True,
                     )
 
-        def y_product(q, h, bank, first):
+        def piece_ps(q, h, t):
+            return row_ps[t][(2 * q + h) % ROW_BANKS]
+
+        def row_pass(q, h, s, step, first):
+            for t in range(2):
+                rows = tile_rows[t]
+                if step == RANK:
+                    weights = bb_mx[rows, HELD if h == t else SENT]
+                    rhs = z_codes[q][rows, :]
+                    rhs_scale = z_scales[q][rows, :]
+                else:
+                    weights = w_half(HELD if step == OWN_K else SENT, h)[rows]
+                    place = t if step == OWN_K else X_SENT
+                    rhs = x_mx[q][rows, place, 0:X_SCALES]
+                    rhs_scale = x_mx[q][rows, place, X_SCALES:X_BYTES]
+                nc.tensor.matmul_mx(
+                    out=piece_ps(q, h, t)[:, s, :],
+                    lhsT=weights[:, s * P * PACK:(s + 1) * P * PACK].bitcast(FP8X4),
+                    lhsT_scale=weights[:, W_SCALES + s * P:W_SCALES + (s + 1) * P],
+                    rhs=rhs.bitcast(FP8X4),
+                    rhs_scale=rhs_scale,
+                    start=(step == first),
+                    stop=(step == RANK),
+                )
+
+        def low_rank_product(h):
             for s in range(2):
-                for step in range(first, 3):
-                    for t in range(2):
-                        rows = half[t]
-                        if step < 2:
-                            held = w_mx[rows, step, h * W_BYTES:(h + 1) * W_BYTES]
-                            slot = t if step == 0 else 2
-                            rhs = x_mx[q][rows, slot, 0:X_SCALES]
-                            rhs_scale = x_mx[q][rows, slot, X_SCALES:X_BYTES]
-                        else:
-                            held = bb_mx[rows, 0 if h == t else 1]
-                            rhs = z_codes[q][rows, :]
-                            rhs_scale = z_scales[q][rows, :]
-                        nc.tensor.matmul_mx(
-                            out=row_ps[t][bank][:, s, :],
-                            lhsT=held[:, s * P * PACK:(s + 1) * P * PACK].bitcast(FP8X4),
-                            lhsT_scale=held[:, W_SCALES + s * P:W_SCALES + (s + 1) * P],
-                            rhs=rhs.bitcast(FP8X4),
-                            rhs_scale=rhs_scale,
-                            start=(step == first),
-                            stop=(step == 2),
-                        )
+                row_pass(0, h, s, RANK, RANK)
 
-        def main_copy(engine, q, h, bank):
-            copy[engine](out=main_sb[q][h][:], in_=main_ps[bank][:])
+        def first_group(q, h, step):
+            row_pass(q, h, 0, step, OWN_K)
 
-        def add(q, h, t, bank):
+        def second_group(q, h):
+            for step in (OWN_K, OTHER_K, RANK):
+                row_pass(q, h, 1, step, OWN_K)
+
+        def main_copy(h):
+            nc.scalar.copy(out=main_sb[h][:], in_=main_ps[:])
+
+        def add(h, t):
             cols = slice(t * NT, (t + 1) * NT)
             nc.vector.tensor_tensor(
-                out=sum_sb[q][h][:, :, cols], in0=row_ps[t][bank][:], in1=main_sb[q][h][:, :, cols], op=ALU.add
+                out=sum_sb[h][:, :, cols], in0=piece_ps(0, h, t)[:], in1=main_sb[h][:, :, cols], op=ALU.add
             )
 
         def relu(engine, dst, src):
@@ -219,99 +242,125 @@ def tile_rows_lora_relu_kernel(tc, x, w, a, bb, out):
             else:
                 nc.scalar.activation(out=dst, in_=src, func=ACT.Relu)
 
+        def relu_sum(engine, h):
+            relu(engine, out_sb[0][h][:], sum_sb[h][:])
+
+        def relu_bank(engine, q, h, t):
+            relu(engine, out_sb[q][h][:, :, t * NT:(t + 1) * NT], piece_ps(q, h, t)[:])
+
         def store(queue, q, h):
             queue.dma_start(out=out_v[:, 2 * h:2 * h + 2, q * CHUNK:(q + 1) * CHUNK], in_=out_sb[q][h][:])
 
-        load_bb(nc.scalar, 1)
         load_bb(nc.sync, 0)
-        load_a(nc.sync)
-        interleave(SCALAR, bb_bf, bb_raw, 0, 256)
-        load_x(nc.sync, 0)
         clear()
-        round_a(VECTOR, 0, 64)
-        load_w(nc.sync, 0, M)
+        load_bb(nc.scalar, 1)
+        load_a()
+        load_x(nc.sync, 0)
+        load_w()
+        load_x(nc.sync, 1)
+        load_x(nc.sync, 2)
+
+        round_bb()
+        round_a()
+        round_x(VECTOR, 0, 0, CHUNK)
+        quantize_x(0)
         quantize_bb()
         quantize_a()
-        interleave(VECTOR, x_bf[0], x_raw[0], 0, 256)
-        quantize_x(0)
-        load_x(nc.sync, 1)
-        round_w(SCALAR, 1, 64, 256)
-        load_x(nc.sync, 2)
-        send(nc.scalar, bb_mx[:, 0, :], bb_mx[:, 1, :], 1)
-        round_w(VECTOR, 0, 0, 256)
+        send_bb(nc.sync, 0)
+        round_w(VECTOR, 0, 0, HALF_M)
+        round_w(SCALAR, 1, W1_ON_VECTOR, HALF_M)
+        z_product(0)
+        send_bb(nc.scalar, 1)
         quantize_w(0)
-        interleave(VECTOR, x_bf[1], x_raw[1], 0, 160)
-        z_product(0, 0)
-        send(nc.sync, bb_mx[:, 0, :], bb_mx[:, 1, :], 0)
-        round_w(VECTOR, 1, 0, 64)
-        interleave(SCALAR, x_bf[1], x_raw[1], 160, 256)
-        load_x(nc.sync, 3)
-        main_product(0, 0, 0)
+        load_x(nc.scalar, 3)
+
+        round_x(VECTOR, 1, 0, X1_ON_VECTOR)
+        round_x(SCALAR, 1, X1_ON_VECTOR, CHUNK)
+        main_product(0)
+        round_z(SCALAR, 0)
+        round_w(VECTOR, 1, 0, W1_ON_VECTOR)
         quantize_x(1)
+        send_w(nc.scalar, 0, 0)
+        main_copy(0)
         quantize_w(1)
-        z_round(SCALAR, 0, 0)
-        main_copy(SCALAR, 0, 0, 0)
+        z_product(1)
         quantize_z(0)
-        interleave(VECTOR, x_bf[2], x_raw[2], 0, 160)
-        interleave(SCALAR, x_bf[2], x_raw[2], 160, 256)
-        z_product(1, 0)
-        send(nc.sync, w_mx[:, 0, :], w_mx[:, 1, :], 0)
-        main_product(0, 1, 0)
-        z_round(SCALAR, 1, 0)
-        y_product(0, 0, 0, 2)
+        send_x(nc.sync, 1, 1)
+        send_w(nc.sync, 0, 1)
+        round_x(VECTOR, 2, 0, X2_ON_VECTOR)
+        send_x(nc.scalar, 1, 0)
+        send_w(nc.sync, 1, 1)
+        round_x(SCALAR, 2, X2_ON_VECTOR, CHUNK)
+        first_group(1, 0, OWN_K)
+        send_w(nc.scalar, 1, 0)
+        low_rank_product(0)
+
         quantize_x(2)
-        y_product(0, 1, 1, 2)
-        z_product(2, 0)
-        add(0, 0, 1, 0)
-        send(nc.sync, w_mx[:, 0, :], w_mx[:, 1, :], 1)
+        main_product(1)
+        round_z(SCALAR, 1)
+        low_rank_product(1)
+        add(0, 1)
+        send_x(nc.sync, 2, 0)
+        add(0, 0)
+        main_copy(1)
+        z_product(2)
+        send_x(nc.sync, 2, 1)
         quantize_z(1)
-        interleave(VECTOR, x_bf[3], x_raw[3], 0, 160)
-        main_copy(SCALAR, 0, 1, 0)
-        interleave(SCALAR, x_bf[3], x_raw[3], 160, 256)
-        add(0, 0, 0, 0)
+        round_x(VECTOR, 3, 0, CHUNK)
+        relu_sum(SCALAR, 0)
+        first_group(1, 1, OWN_K)
+        first_group(1, 0, OTHER_K)
+        first_group(1, 0, RANK)
+        add(1, 1)
+        second_group(1, 0)
+        round_z(SCALAR, 2)
         quantize_x(3)
-        send(nc.sync, x_mx[2][:, 1, :], x_mx[2][:, 2, :], 1)
-        z_round(SCALAR, 2, 0)
-        main_product(1, 0, 0)
-        send(nc.sync, x_mx[2][:, 0, :], x_mx[2][:, 2, :], 0)
-        main_copy(SCALAR, 1, 0, 0)
-        send(nc.sync, x_mx[3][:, 0, :], x_mx[3][:, 2, :], 0)
-        add(0, 1, 0, 1)
-        send(nc.sync, x_mx[3][:, 1, :], x_mx[3][:, 2, :], 1)
-        relu(SCALAR, out_sb[0][0][:], sum_sb[0][0][:])
-        add(0, 1, 1, 1)
-        y_product(1, 0, 2, 2)
-        quantize_z(2)
-        relu(VECTOR, out_sb[0][1][:], sum_sb[0][1][:])
-        y_product(1, 1, 0, 2)
-        add(1, 0, 1, 2)
-        z_product(3, 0)
-        add(1, 0, 0, 2)
-        relu(VECTOR, out_sb[1][0][:], sum_sb[1][0][:])
-        z_round(SCALAR, 3, 0)
-        main_product(1, 1, 0)
-        store(nc.sync, 0, 1)
-        y_product(2, 0, 1, 0)
-        main_copy(SCALAR, 1, 1, 0)
+
         store(nc.sync, 0, 0)
-        quantize_z(3)
+        first_group(1, 1, OTHER_K)
+        first_group(1, 1, RANK)
+        second_group(1, 1)
+        relu_bank(SCALAR, 1, 0, 0)
+        relu_bank(VECTOR, 1, 0, 1)
+        send_x(nc.sync, 3, 1)
+        z_product(3)
+        send_x(nc.scalar, 3, 0)
+        add(1, 0)
+        relu_bank(SCALAR, 1, 1, 1)
+        quantize_z(2)
         store(nc.sync, 1, 0)
-        relu(SCALAR, out_sb[2][0][:, :, 1 * NT:2 * NT], row_ps[1][1][:])
-        relu(SCALAR, out_sb[2][0][:, :, 0 * NT:1 * NT], row_ps[0][1][:])
-        add(1, 1, 0, 0)
-        add(1, 1, 1, 0)
-        y_product(2, 1, 2, 0)
-        relu(SCALAR, out_sb[2][1][:, :, 0 * NT:1 * NT], row_ps[0][2][:])
-        relu(VECTOR, out_sb[1][1][:], sum_sb[1][1][:])
-        store(nc.sync, 2, 0)
-        y_product(3, 0, 0, 0)
-        relu(VECTOR, out_sb[3][0][:, :, 1 * NT:2 * NT], row_ps[1][0][:])
-        y_product(3, 1, 1, 0)
+        relu_bank(SCALAR, 1, 1, 0)
+        relu_sum(VECTOR, 1)
+
+        first_group(2, 0, OWN_K)
+        first_group(2, 0, OTHER_K)
+        first_group(2, 0, RANK)
+        round_z(VECTOR, 3)
         store(nc.scalar, 1, 1)
-        relu(SCALAR, out_sb[2][1][:, :, 1 * NT:2 * NT], row_ps[1][2][:])
-        relu(SCALAR, out_sb[3][1][:, :, 1 * NT:2 * NT], row_ps[1][1][:])
-        store(nc.sync, 2, 1)
-        relu(VECTOR, out_sb[3][0][:, :, 0 * NT:1 * NT], row_ps[0][0][:])
+        second_group(2, 0)
+        store(nc.scalar, 0, 1)
+        first_group(2, 1, OWN_K)
+        first_group(3, 0, OWN_K)
+        first_group(2, 1, OTHER_K)
+        first_group(2, 1, RANK)
+        second_group(2, 1)
+        relu_bank(SCALAR, 2, 0, 0)
+        relu_bank(VECTOR, 2, 0, 1)
+        quantize_z(3)
+        first_group(3, 1, OWN_K)
+        store(nc.scalar, 2, 0)
+        relu_bank(VECTOR, 2, 1, 0)
+        first_group(3, 0, OTHER_K)
+        relu_bank(SCALAR, 2, 1, 1)
+        first_group(3, 0, RANK)
+        second_group(3, 0)
+        first_group(3, 1, OTHER_K)
+        store(nc.scalar, 2, 1)
+        first_group(3, 1, RANK)
+        second_group(3, 1)
+        relu_bank(VECTOR, 3, 0, 0)
+        relu_bank(SCALAR, 3, 0, 1)
+        relu_bank(SCALAR, 3, 1, 0)
+        relu_bank(VECTOR, 3, 1, 1)
         store(nc.sync, 3, 0)
-        relu(VECTOR, out_sb[3][1][:, :, 0 * NT:1 * NT], row_ps[0][1][:])
         store(nc.sync, 3, 1)

from contextlib import ExitStack

import concourse.mybir as mybir

K, R, M, N = 512, 256, 512, 1024
FLOPS = 2 * N * (K * M + K * R + R * M)

F32 = mybir.dt.float32
BF16 = mybir.dt.bfloat16
I32 = mybir.dt.int32
U32 = mybir.dt.uint32
U8 = mybir.dt.uint8
FP8X4 = mybir.dt.float8_e4m3fn_x4
ALU = mybir.AluOpType
ACT = mybir.ActivationFunctionType

P = 128
PACK = 4
ROWS = 64
NT = 128
CHUNK = 2 * NT
CHUNKS = N // CHUNK
HALF_M = M // 2

W_SCALES = HALF_M * PACK
W_BYTES = W_SCALES + HALF_M
X_SCALES = NT * PACK
X_BYTES = X_SCALES + NT

HELD, SENT = 0, 1
X_SENT = 2
OWN_K, OTHER_K, RANK = 0, 1, 2
ROW_BANKS = 3
VECTOR, SCALAR = 0, 1

W1_ON_VECTOR = 64
X1_ON_VECTOR = 176
X2_ON_VECTOR = 192


def tile_rows_lora_relu_kernel(tc, x, w, a, bb, out):
    nc = tc.nc
    copy = (nc.vector.tensor_copy, nc.scalar.copy)
    tile_rows = (slice(0, ROWS), slice(ROWS, P))

    with ExitStack() as ctx:
        sb = ctx.enter_context(tc.tile_pool(name="sb", bufs=1))
        ps = ctx.enter_context(tc.psum_pool(name="ps", bufs=1))
        ctx.enter_context(tc.manual_schedule())

        bb_raw = sb.tile([P, PACK, HALF_M], F32, name="bb_raw")
        bb_bf = sb.tile([P, HALF_M, PACK], BF16, name="bb_bf", align_bytes=64)
        bb_mx = sb.tile([P, 2, W_BYTES], U8, name="bb_mx", align_bytes=64)
        a_raw = sb.tile([P, PACK, R], F32, name="a_raw")
        a_bf = sb.tile([P, PACK, ROWS, PACK], BF16, name="a_bf", align_bytes=64)
        a_codes = sb.tile([P, (2 * PACK + 1) * ROWS], U32, name="a_codes", align_bytes=64)
        a_scales = sb.tile([P, (2 * PACK + 1) * ROWS], U8, name="a_scales", align_bytes=64)
        w_raw = sb.tile([P, PACK, M], F32, name="w_raw")
        w_bf = [sb.tile([P, HALF_M, PACK], BF16, name="w_bf%d" % h, align_bytes=64) for h in range(2)]
        w_mx = sb.tile([P, 2, 2 * W_BYTES], U8, name="w_mx", align_bytes=64)
        x_raw = [sb.tile([P, PACK, CHUNK], F32, name="x_raw%d" % q) for q in range(CHUNKS)]
        x_bf = [sb.tile([P, CHUNK, PACK], BF16, name="x_bf%d" % q, align_bytes=64) for q in range(CHUNKS)]
        x_mx = [sb.tile([P, 3, X_BYTES], U8, name="x_mx%d" % q, align_bytes=64) for q in range(CHUNKS)]
        z_bf = [sb.tile([P, NT, PACK], BF16, name="z_bf%d" % q, align_bytes=64) for q in range(CHUNKS)]
        z_codes = [sb.tile([P, NT], U32, name="z_codes%d" % q, align_bytes=64) for q in range(CHUNKS)]
        z_scales = [sb.tile([P, NT], U8, name="z_scales%d" % q, align_bytes=64) for q in range(CHUNKS)]
        main_sb = [sb.tile([P, 2, CHUNK], F32, name="main_sb%d" % h) for h in range(2)]
        sum_sb = [sb.tile([P, 2, CHUNK], F32, name="sum_sb%d" % h) for h in range(2)]
        out_sb = [[sb.tile([P, 2, CHUNK], F32, name="out_sb%d_%d" % (q, h)) for h in range(2)] for q in range(CHUNKS)]

        z_ps = ps.tile([P, PACK, NT], F32, name="z_ps")
        main_ps = ps.tile([P, 2, CHUNK], F32, name="main_ps")
        row_ps = [[ps.tile([P, 2, NT], F32, name="row_ps%d_%d" % (t, b)) for b in range(ROW_BANKS)] for t in range(2)]

        out_v = out.rearrange("(mt p) n -> p mt n", p=P)
        bb_v = bb.rearrange("(p j) m -> p j m", j=PACK)
        x_v = x.rearrange("(p j) n -> p j n", j=PACK)

        def load_a():
            nc.sync.dma_start(out=a_raw[:], in_=a.rearrange("(p j) r -> p j r", j=PACK))

        def load_w():
            nc.sync.dma_start(out=w_raw[:], in_=w.rearrange("(p j) m -> p j m", j=PACK))

        def load_bb(queue, t):
            queue.dma_start(out=bb_raw[tile_rows[t]], in_=bb_v[:, :, t * HALF_M:(t + 1) * HALF_M])

        def load_x(queue, q):
            queue.dma_start(out=x_raw[q][:], in_=x_v[:, :, q * CHUNK:(q + 1) * CHUNK])

        def clear():
            nc.vector.memset(a_codes[:], 0)
            nc.vector.memset(a_scales[:], 127)
            nc.vector.memset(bb_mx[:, HELD, W_SCALES:W_BYTES].bitcast(I32), 0)
            for h in range(2):
                nc.vector.memset(w_mx[:, HELD, h * W_BYTES + W_SCALES:(h + 1) * W_BYTES].bitcast(I32), 0)
            for q in range(1, CHUNKS):
                nc.vector.memset(x_mx[q][:, 0:X_SENT, X_SCALES:X_BYTES].bitcast(I32), 0)

        def interleave(engine, dst, src, lo, hi):
            copy[engine](
                out=dst[:, lo:hi, :].rearrange("p (c i) j -> p c j i", i=4),
                in_=src[:, :, lo:hi].rearrange("p j (c i) -> p c j i", i=4),
            )

        def round_bb():
            interleave(VECTOR, bb_bf, bb_raw, 0, HALF_M)

        def round_w(engine, h, lo, hi):
            interleave(engine, w_bf[h], w_raw[:, :, h * HALF_M:(h + 1) * HALF_M], lo, hi)

        def round_x(engine, q, lo, hi):
            interleave(engine, x_bf[q], x_raw[q], lo, hi)

        def round_a():
            nc.vector.tensor_copy(
                out=a_bf[:].rearrange("p i s j -> p s j i"),
                in_=a_raw[:].rearrange("p j (s i) -> p s j i", i=PACK),
            )

        def quantize(codes, scales, grouped):
            nc.vector.quantize_mx(out=codes.bitcast(FP8X4), scales=scales, in_=grouped)

        def quantize_a():
            for i in range(PACK):
                strip = slice((2 * i + 1) * ROWS, (2 * i + 2) * ROWS)
                quantize(a_codes[:, strip], a_scales[:, strip], a_bf[:, i].rearrange("p s j -> p (s j)"))

        def quantize_bb():
            held = bb_mx[:, HELD]
            quantize(held[:, 0:W_SCALES], held[:, W_SCALES:W_BYTES], bb_bf[:].rearrange("p m j -> p (m j)"))

        def w_half(place, h):
            return w_mx[:, place, h * W_BYTES:(h + 1) * W_BYTES]

        def quantize_w(h):
            held = w_half(HELD, h)
            quantize(held[:, 0:W_SCALES], held[:, W_SCALES:W_BYTES], w_bf[h][:].rearrange("p m j -> p (m j)"))

        def quantize_x(q):
            for t in range(2):
                quantize(
                    x_mx[q][:, t, 0:X_SCALES],
                    x_mx[q][:, t, X_SCALES:X_BYTES],
                    x_bf[q][:, t * NT:(t + 1) * NT, :].rearrange("p n j -> p (n j)"),
                )

        def quantize_z(q):
            quantize(z_codes[q][:], z_scales[q][:], z_bf[q][:].rearrange("p n i -> p (n i)"))

        def send(queue, src, dst, t):
            queue.dma_start(out=dst[tile_rows[t]].bitcast(I32), in_=src[tile_rows[1 - t]].bitcast(I32))

        def send_bb(queue, t):
            send(queue, bb_mx[:, HELD, :], bb_mx[:, SENT, :], t)

        def send_w(queue, h, t):
            send(queue, w_half(HELD, h), w_half(SENT, h), t)

        def send_x(queue, q, t):
            send(queue, x_mx[q][:, t, :], x_mx[q][:, X_SENT, :], t)

        def z_product(q):
            for i in range(PACK):
                for t in range(2):
                    window = slice((2 * i + 1 - t) * ROWS, (2 * i + 3 - t) * ROWS)
                    nc.tensor.matmul_mx(
                        out=z_ps[:, i, :],
                        lhsT=a_codes[:, window].bitcast(FP8X4),
                        lhsT_scale=a_scales[:, window],
                        rhs=x_mx[q][:, t, 0:X_SCALES].bitcast(FP8X4),
                        rhs_scale=x_mx[q][:, t, X_SCALES:X_BYTES],
                        start=(t == 0),
                        stop=(t == 1),
                    )

        def round_z(engine, q):
            copy[engine](out=z_bf[q][:], in_=z_ps[:].rearrange("p i n -> p n i"))

        def main_product(h):
            held = w_half(HELD, h)
            for s in range(2):
                for t in range(2):
                    nc.tensor.matmul_mx(
                        out=main_ps[:, s, t * NT:(t + 1) * NT],
                        lhsT=held[:, s * P * PACK:(s + 1) * P * PACK].bitcast(FP8X4),
                        lhsT_scale=held[:, W_SCALES + s * P:W_SCALES + (s + 1) * P],
                        rhs=x_mx[0][:, t, 0:X_SCALES].bitcast(FP8X4),
                        rhs_scale=x_mx[0][:, t, X_SCALES:X_BYTES],
                        start=True,
                        stop=True,
                    )

        def piece_ps(q, h, t):
            return row_ps[t][(2 * q + h) % ROW_BANKS]

        def row_pass(q, h, s, step, first):
            for t in range(2):
                rows = tile_rows[t]
                if step == RANK:
                    weights = bb_mx[rows, HELD if h == t else SENT]
                    rhs = z_codes[q][rows, :]
                    rhs_scale = z_scales[q][rows, :]
                else:
                    weights = w_half(HELD if step == OWN_K else SENT, h)[rows]
                    place = t if step == OWN_K else X_SENT
                    rhs = x_mx[q][rows, place, 0:X_SCALES]
                    rhs_scale = x_mx[q][rows, place, X_SCALES:X_BYTES]
                nc.tensor.matmul_mx(
                    out=piece_ps(q, h, t)[:, s, :],
                    lhsT=weights[:, s * P * PACK:(s + 1) * P * PACK].bitcast(FP8X4),
                    lhsT_scale=weights[:, W_SCALES + s * P:W_SCALES + (s + 1) * P],
                    rhs=rhs.bitcast(FP8X4),
                    rhs_scale=rhs_scale,
                    start=(step == first),
                    stop=(step == RANK),
                )

        def low_rank_product(h):
            for s in range(2):
                row_pass(0, h, s, RANK, RANK)

        def first_group(q, h, step):
            row_pass(q, h, 0, step, OWN_K)

        def second_group(q, h):
            for step in (OWN_K, OTHER_K, RANK):
                row_pass(q, h, 1, step, OWN_K)

        def main_copy(h):
            nc.scalar.copy(out=main_sb[h][:], in_=main_ps[:])

        def add(h, t):
            cols = slice(t * NT, (t + 1) * NT)
            nc.vector.tensor_tensor(
                out=sum_sb[h][:, :, cols], in0=piece_ps(0, h, t)[:], in1=main_sb[h][:, :, cols], op=ALU.add
            )

        def relu(engine, dst, src):
            if engine == VECTOR:
                nc.vector.tensor_scalar(out=dst, in0=src, scalar1=0.0, scalar2=None, op0=ALU.max)
            else:
                nc.scalar.activation(out=dst, in_=src, func=ACT.Relu)

        def relu_sum(engine, h):
            relu(engine, out_sb[0][h][:], sum_sb[h][:])

        def relu_bank(engine, q, h, t):
            relu(engine, out_sb[q][h][:, :, t * NT:(t + 1) * NT], piece_ps(q, h, t)[:])

        def store(queue, q, h):
            queue.dma_start(out=out_v[:, 2 * h:2 * h + 2, q * CHUNK:(q + 1) * CHUNK], in_=out_sb[q][h][:])

        load_bb(nc.sync, 0)
        clear()
        load_bb(nc.scalar, 1)
        load_a()
        load_x(nc.sync, 0)
        load_w()
        load_x(nc.sync, 1)
        load_x(nc.sync, 2)

        round_bb()
        round_a()
        round_x(VECTOR, 0, 0, CHUNK)
        quantize_x(0)
        quantize_bb()
        quantize_a()
        send_bb(nc.sync, 0)
        round_w(VECTOR, 0, 0, HALF_M)
        round_w(SCALAR, 1, W1_ON_VECTOR, HALF_M)
        z_product(0)
        send_bb(nc.scalar, 1)
        quantize_w(0)
        load_x(nc.scalar, 3)

        round_x(VECTOR, 1, 0, X1_ON_VECTOR)
        round_x(SCALAR, 1, X1_ON_VECTOR, CHUNK)
        main_product(0)
        round_z(SCALAR, 0)
        round_w(VECTOR, 1, 0, W1_ON_VECTOR)
        quantize_x(1)
        send_w(nc.scalar, 0, 0)
        main_copy(0)
        quantize_w(1)
        z_product(1)
        quantize_z(0)
        send_x(nc.sync, 1, 1)
        send_w(nc.sync, 0, 1)
        round_x(VECTOR, 2, 0, X2_ON_VECTOR)
        send_x(nc.scalar, 1, 0)
        send_w(nc.sync, 1, 1)
        round_x(SCALAR, 2, X2_ON_VECTOR, CHUNK)
        first_group(1, 0, OWN_K)
        send_w(nc.scalar, 1, 0)
        low_rank_product(0)

        quantize_x(2)
        main_product(1)
        round_z(SCALAR, 1)
        low_rank_product(1)
        add(0, 1)
        send_x(nc.sync, 2, 0)
        add(0, 0)
        main_copy(1)
        z_product(2)
        send_x(nc.sync, 2, 1)
        quantize_z(1)
        round_x(VECTOR, 3, 0, CHUNK)
        relu_sum(SCALAR, 0)
        first_group(1, 1, OWN_K)
        first_group(1, 0, OTHER_K)
        first_group(1, 0, RANK)
        add(1, 1)
        second_group(1, 0)
        round_z(SCALAR, 2)
        quantize_x(3)

        store(nc.sync, 0, 0)
        first_group(1, 1, OTHER_K)
        first_group(1, 1, RANK)
        second_group(1, 1)
        relu_bank(SCALAR, 1, 0, 0)
        relu_bank(VECTOR, 1, 0, 1)
        send_x(nc.sync, 3, 1)
        z_product(3)
        send_x(nc.scalar, 3, 0)
        add(1, 0)
        relu_bank(SCALAR, 1, 1, 1)
        quantize_z(2)
        store(nc.sync, 1, 0)
        relu_bank(SCALAR, 1, 1, 0)
        relu_sum(VECTOR, 1)

        first_group(2, 0, OWN_K)
        first_group(2, 0, OTHER_K)
        first_group(2, 0, RANK)
        round_z(VECTOR, 3)
        store(nc.scalar, 1, 1)
        second_group(2, 0)
        store(nc.scalar, 0, 1)
        first_group(2, 1, OWN_K)
        first_group(3, 0, OWN_K)
        first_group(2, 1, OTHER_K)
        first_group(2, 1, RANK)
        second_group(2, 1)
        relu_bank(SCALAR, 2, 0, 0)
        relu_bank(VECTOR, 2, 0, 1)
        quantize_z(3)
        first_group(3, 1, OWN_K)
        store(nc.scalar, 2, 0)
        relu_bank(VECTOR, 2, 1, 0)
        first_group(3, 0, OTHER_K)
        relu_bank(SCALAR, 2, 1, 1)
        first_group(3, 0, RANK)
        second_group(3, 0)
        first_group(3, 1, OTHER_K)
        store(nc.scalar, 2, 1)
        first_group(3, 1, RANK)
        second_group(3, 1)
        relu_bank(VECTOR, 3, 0, 0)
        relu_bank(SCALAR, 3, 0, 1)
        relu_bank(SCALAR, 3, 1, 0)
        relu_bank(VECTOR, 3, 1, 1)
        store(nc.sync, 3, 0)
        store(nc.sync, 3, 1)
